import numpy as np
import ml_dtypes


def mxq(x, axis, fmt="e4m3"):
    dtype, down = {"e4m3": (ml_dtypes.float8_e4m3fn, 7), "e5m2": (ml_dtypes.float8_e5m2, 14)}[fmt]
    v = np.moveaxis(np.asarray(x, np.float32).astype(ml_dtypes.bfloat16).astype(np.float64), axis, -1)
    blocks = v.reshape(v.shape[:-1] + (-1, 32))
    amax = np.abs(blocks).max(-1, keepdims=True)
    byte = np.maximum(np.where(amax > 0, np.frexp(amax)[1] - 1 + 127, 0) - down, 1)
    scale = np.exp2(byte - 127.0)
    codes = (blocks / scale).astype(np.float32).astype(dtype).astype(np.float64)
    return np.moveaxis((codes * scale).reshape(v.shape), -1, axis)


WIDE = False


def mx_kscale(k):
    if not WIDE:
        return np.ones(k)
    levels = np.array([10, -10, 5, -5, 0])
    if k % 512:
        return np.exp2(np.random.permutation(np.resize(levels, k // 32))).repeat(32)
    a = np.empty((k // 512, 16))
    for p in range(k // 512):
        a[p, :8] = np.random.permutation(np.resize(levels, 8))
        for g in range(8):
            far = levels[np.abs(levels - a[p, g]) >= 10]
            a[p, g + 8] = far[np.random.randint(len(far))]
    return np.exp2(a.ravel()).repeat(32)


def f64(x):
    return np.asarray(x).astype(np.float64)


def striped(idx):
    return np.tile(idx.reshape(-1, 16).T, (8, 1)).astype(np.uint16)


def unstriped(offs):
    return offs[:16].T.reshape(-1).astype(np.int64)


E2M1 = np.array([0.0, 0.5, 1.0, 1.5, 2.0, 3.0, 4.0, 6.0, -0.0, -0.5, -1.0, -1.5, -2.0, -3.0, -4.0, -6.0])


def pack_weight(w, fmt):
    k, n = w.shape
    w = f64(np.asarray(w, np.float32).astype(ml_dtypes.bfloat16)).reshape(k // 32, 32, n)
    amax = np.abs(w).max(1)
    if fmt == "e4m3":
        byte = np.frexp(amax)[1] - 1 + 127 - 7
    else:
        mant, ex = np.frexp(amax / 6.0)
        byte = np.where(mant > 0.5, ex, ex - 1) + 127
    byte = np.clip(np.where(amax > 0, byte, 1), 1, 254)
    scaled = (w * np.exp2(127.0 - byte)[:, None, :]).reshape(k, n).astype(np.float32)
    by_word = np.ascontiguousarray(scaled.reshape(k // 512, 128, 4, n).transpose(0, 1, 3, 2))
    if fmt == "e4m3":
        words = by_word.astype(ml_dtypes.float8_e4m3fn).view(np.uint8)
    else:
        c = by_word.astype(ml_dtypes.float4_e2m1fn).view(np.uint8) & 0xF
        words = (c[..., 0::2] | (c[..., 1::2] << 4)).reshape(k // 512, 128, 2 * n)
    return np.ascontiguousarray(words), np.ascontiguousarray(byte.astype(np.uint8).reshape(k // 512, 16, n))


def unpack_weight(words, scales, fmt):
    g, _, n = scales.shape
    words = np.ascontiguousarray(words).reshape(g, 128, n, -1)
    if fmt == "e4m3":
        vals = words.view(ml_dtypes.float8_e4m3fn).astype(np.float64)
    else:
        nib = np.empty((g, 128, n, 4), np.uint8)
        nib[..., 0::2] = words & 0xF
        nib[..., 1::2] = words >> 4
        vals = E2M1[nib]
    vals = vals * np.repeat(np.exp2(scales.astype(np.float64) - 127.0), 8, axis=1)[..., None]
    return vals.transpose(0, 1, 3, 2).reshape(g * 512, n)


def gelu(v):
    return 0.5 * v * (1.0 + np.tanh(np.sqrt(2.0 / np.pi) * (v + 0.044715 * v**3)))


K, T, G, C1, E, C2, H = 1024, 1024, 2, 512, 4, 256, 512
N = 256


def by_expert(wq, xq, E, C):
    return np.concatenate([wq[e].T @ xq[:, e * C:(e + 1) * C] for e in range(E)], axis=1)


def setup_inputs():
    n = np.random.standard_normal
    s = mx_kscale(K)
    u = mx_kscale(H)
    slots1 = np.random.permutation(T)
    slots2 = np.concatenate([q * C1 + np.random.permutation(C1) for q in range(G)])
    x = pack_weight(n((K, T)) * s[:, None], "e4m3")
    wg = [pack_weight(m, "e4m3") for m in n((G, K, H)) / np.sqrt(K) / s[None, :, None] * u]
    return {
        "x_words": x[0],
        "x_scales": x[1],
        "wg_words": np.stack([m[0] for m in wg]),
        "wg_scales": np.stack([m[1] for m in wg]),
        "we": (n((E, H, N)) / np.sqrt(H) / u[None, :, None]).astype(np.float32),
        "gate": (np.tile(np.random.uniform(0.2, 1.0, T), (128, 1))).astype(np.float32),
        "offs": striped(slots1),
        "offs2": striped(slots2),
        "dst": striped(slots1[slots2]),
    }


def reference(x_words, x_scales, wg_words, wg_scales, we, gate, offs, offs2, dst):
    wg = np.stack([unpack_weight(wg_words[e], wg_scales[e], "e4m3") for e in range(G)])
    weq = mxq(f64(we), 1, "e4m3")
    idx, idx2 = unstriped(offs), unstriped(offs2)
    xq = unpack_weight(x_words, x_scales, "e4m3")[:, idx]
    a = gelu(by_expert(wg, xq, G, C1))
    y = by_expert(weq, mxq(a[:, idx2], 0, "e4m3"), E, C2)
    out = np.zeros((N, T))
    out[:, unstriped(dst)] = f64(gate[:1]) * y
    return out

@@ -1,0 +1,230 @@
+from contextlib import ExitStack
+
+import concourse.mybir as mybir
+
+K, T, G, C1, E, C2, H, N = 1024, 1024, 2, 512, 4, 256, 512, 256
+FLOPS = 2 * T * (K * H + H * N)
+
+F32 = mybir.dt.float32
+BF16 = mybir.dt.bfloat16
+I32 = mybir.dt.int32
+U32 = mybir.dt.uint32
+U16 = mybir.dt.uint16
+U8 = mybir.dt.uint8
+FP8X4 = mybir.dt.float8_e4m3fn_x4
+GELU = mybir.ActivationFunctionType.Gelu_apprx_tanh
+COPY = mybir.ActivationFunctionType.Copy
+MULT = mybir.AluOpType.mult
+
+P = 128
+PASSES = 2
+X_PLANE = 8
+
+
+def tile_moe_hie_gelu_kernel(
+    tc, x_words, x_scales, wg_words, wg_scales, we, gate, offs, offs2, dst, out
+):
+    nc = tc.nc
+    with ExitStack() as ctx:
+        sb = ctx.enter_context(tc.tile_pool(name="sb", bufs=1))
+        ps = ctx.enter_context(tc.psum_pool(name="ps", bufs=8))
+
+        def tile(shape, dtype, name):
+            return sb.tile(shape, dtype, name=name, align_bytes=64)
+
+        idx1 = sb.tile([P, T // 16], U16, name="idx1")
+        idx2 = sb.tile([P, T // 16], U16, name="idx2")
+        ret = sb.tile([P, T // 16], U16, name="ret")
+
+        xs = tile([P, T], U8, "xs")
+        wgs = tile([P, H], U8, "wgs")
+        nc.vector.memset(xs[:].bitcast(I32), 0)
+        nc.gpsimd.memset(wgs[:].bitcast(I32), 0)
+
+        nc.sync.dma_start(idx1[:], offs)
+        for q in range(4):
+            nc.scalar.dma_start(
+                xs[32 * q + X_PLANE : 32 * q + X_PLANE + 8, :].bitcast(I32),
+                x_scales[:, 4 * q : 4 * q + 4, :].bitcast(I32),
+            )
+
+        xw = [tile([P, T], I32, f"xw{s}") for s in range(PASSES)]
+        wg_raw = [tile([P, PASSES * H], I32, f"wg_raw{f}") for f in range(G)]
+        we_raw = [tile([P, 4, N], F32, f"we_raw{e}") for e in range(E)]
+        g = tile([P, T], F32, "g")
+
+        def load_wg(f):
+            nc.sync.dma_start(
+                wg_raw[f][:].rearrange("p (s i) -> p s i", s=PASSES),
+                wg_words[f].rearrange("s p i d -> p s (i d)").bitcast(I32),
+            )
+
+        def load_we(e):
+            nc.sync.dma_start(we_raw[e][:], we[e].rearrange("(p j) n -> p j n", j=4))
+
+        for s in range(PASSES):
+            nc.sync.dma_start(xw[s][:], x_words[s].rearrange("p t d -> p (t d)").bitcast(I32))
+        load_wg(0)
+        wgs_rows = wg_scales.rearrange("f s b i -> (f s) b i")
+        for q in range(4):
+            nc.sync.dma_start(
+                wgs[32 * q : 32 * q + 16, :].bitcast(I32),
+                wgs_rows[:, 4 * q : 4 * q + 4, :].bitcast(I32),
+            )
+        warm_in = tile([P, 1], F32, "warm_in")
+        warm_out = tile([P, 1], F32, "warm_out")
+        nc.vector.memset(warm_in[:], 0.0)
+        nc.scalar.activation(warm_out[:], warm_in[:], GELU)
+
+        load_we(0)
+        load_wg(1)
+        nc.sync.dma_start(idx2[:], offs2)
+        load_we(1)
+        nc.sync.dma_start(ret[:], dst)
+        nc.sync.dma_start(g[:], gate)
+        load_we(2)
+        load_we(3)
+
+        xs_g = [tile([P, C1], U8, f"xs_g{f}") for f in range(G)]
+        xw_g = [[tile([P, C1], U32, f"xw_g{f}{s}") for s in range(PASSES)] for f in range(G)]
+        wg_p = [tile([P, PASSES * H], I32, f"wg_p{f}") for f in range(G)]
+        wgs_p = tile([P, H], U8, "wgs_p")
+        a = tile([P, 4 * T], BF16, "a")
+        we_bf = [tile([P, N, 4], BF16, f"we_bf{e}") for e in range(E)]
+        we_q = [tile([P, N], U32, f"we_q{e}") for e in range(E)]
+        we_s = [tile([P, N], U8, f"we_s{e}") for e in range(E)]
+        a_bf = [tile([P, C2, 4], BF16, f"a_bf{e}") for e in range(E)]
+        a_q = [tile([P, C2], U32, f"a_q{e}") for e in range(E)]
+        a_s = [tile([P, C2], U8, f"a_s{e}") for e in range(E)]
+        y = [tile([P, 2, C2], F32, f"y{e}") for e in range(E)]
+        res = [tile([P, T], F32, f"res{r}") for r in range(2)]
+
+        def entries(lst, start, count):
+            return lst[:, start // 16 : (start + count) // 16]
+
+        def gather_scales(f):
+            nc.vector.tensor_copy(xs_g[f][:], xs[:].indirect(entries(idx1, f * C1, C1)))
+
+        def gather_words(f, s, start, count):
+            nc.vector.tensor_copy(
+                xw_g[f][s][:, start : start + count],
+                xw[s][:].bitcast(U32).indirect(entries(idx1, f * C1 + start, count)),
+            )
+
+        def permute_wg(f):
+            nc.vector.tensor_copy(
+                wg_p[f][:].rearrange("p (t q l) -> p q t l", t=4, l=4),
+                wg_raw[f][:].rearrange("p (q l t) -> p q t l", t=4, l=4),
+            )
+
+        def first_pass(f, s, t, acc, start, count):
+            col = (t * PASSES + s) * P
+            nc.tensor.matmul_mx(
+                out=acc,
+                lhsT=wg_p[f][:, col : col + P].bitcast(FP8X4),
+                lhsT_scale=wgs_p[4 * (PASSES * f + s) :, t * P : (t + 1) * P],
+                rhs=xw_g[f][s][:, start : start + count].bitcast(FP8X4),
+                rhs_scale=xs_g[f][X_PLANE + 4 * s :, start : start + count],
+                start=(s == 0),
+                stop=(s == PASSES - 1),
+            )
+
+        def cast_we(e):
+            nc.scalar.copy(
+                we_bf[e][:].rearrange("p (c i) j -> p c j i", i=4),
+                we_raw[e][:].rearrange("p j (c i) -> p c j i", i=4),
+            )
+
+        def quantize(codes, scales, values):
+            nc.vector.quantize_mx(
+                out=codes[:].bitcast(FP8X4), scales=scales[:], in_=values[:].rearrange("p n j -> p (n j)")
+            )
+
+        def gather_pairs(e):
+            for u in range(2):
+                words = a_bf[e][:].rearrange("p n j -> p (n j)").bitcast(U32)
+                nc.vector.tensor_copy(
+                    words[:, u :: 2],
+                    a[:, u * 2 * C1 : (u + 1) * 2 * C1].bitcast(U32).indirect(entries(idx2, e * C2, C2)),
+                )
+
+        def gather_plane(e, t):
+            lo = 3 * C1 + t * C1
+            nc.scalar.activation(
+                a_bf[e][:, :, t], a[:, lo : lo + T].indirect(entries(idx2, e * C2, C2)), COPY
+            )
+
+        def second(e):
+            acc = ps.tile([P, 2, C2], F32, name="acc", tag="bank")
+            for r in range(2):
+                nc.tensor.matmul_mx(
+                    out=acc[:, r, :],
+                    lhsT=we_q[e][:, r * P : (r + 1) * P].bitcast(FP8X4),
+                    lhsT_scale=we_s[e][:, r * P : (r + 1) * P],
+                    rhs=a_q[e][:].bitcast(FP8X4),
+                    rhs_scale=a_s[e][:],
+                    start=True,
+                    stop=True,
+                )
+            nc.scalar.copy(y[e][:], acc[:])
+
+        def scatter(e, r):
+            nc.vector.tensor_tensor(
+                res[r][:].indirect(entries(ret, e * C2, C2)), y[e][:, r, :], g[:, e * C2 : (e + 1) * C2], MULT
+            )
+
+        gather_scales(0)
+        gather_scales(1)
+        gather_words(0, 0, 0, C1)
+        gather_words(0, 1, 0, C2)
+        nc.vector.tensor_copy(
+            wgs_p[:].rearrange("p (t m) -> p t m", t=4), wgs[:].rearrange("p (m t) -> p t m", t=4)
+        )
+        permute_wg(0)
+        gather_words(0, 1, C2, C2)
+        cast_we(0)
+        for h in range(2):
+            for u in range(2):
+                acc = ps.tile([P, 2, C2], F32, name="acc", tag="bank")
+                for c in range(2):
+                    for s in range(PASSES):
+                        first_pass(0, s, 2 * u + c, acc[:, c, :], h * C2, C2)
+                lo = u * 2 * C1 + h * 2 * C2
+                nc.scalar.activation(
+                    a[:, lo : lo + 2 * C2].rearrange("p (n c) -> p n c", c=2),
+                    acc[:].rearrange("p c n -> p n c"),
+                    GELU,
+                )
+        gather_words(1, 0, 0, C1)
+        permute_wg(1)
+        gather_words(1, 1, 0, C1)
+        cast_we(1)
+        banks = [ps.tile([P, C1], F32, name="acc", tag="bank") for t in range(4)]
+        for s in range(PASSES):
+            for t in range(4):
+                first_pass(1, s, t, banks[t][:], 0, C1)
+        quantize(we_q[0], we_s[0], we_bf[0])
+        gather_pairs(0)
+        quantize(we_q[1], we_s[1], we_bf[1])
+        quantize(a_q[0], a_s[0], a_bf[0])
+        for t in range(4):
+            lo = 4 * C1 + t * C1
+            nc.scalar.activation(a[:, lo : lo + C1], banks[t][:], GELU)
+        second(0)
+        gather_pairs(1)
+        scatter(0, 0)
+        quantize(a_q[1], a_s[1], a_bf[1])
+        second(1)
+        scatter(0, 1)
+        for e in range(2, E):
+            cast_we(e)
+            for t in range(4):
+                gather_plane(e, t)
+            quantize(we_q[e], we_s[e], we_bf[e])
+            quantize(a_q[e], a_s[e], a_bf[e])
+            second(e)
+            scatter(e - 1, 0)
+            scatter(e - 1, 1)
+        for r in range(2):
+            scatter(E - 1, r)
+            nc.sync.dma_start(out[r * P : (r + 1) * P, :], res[r][:])

@@ -15,10 +15,34 @@ FP8X4 = mybir.dt.float8_e4m3fn_x4
 GELU = mybir.ActivationFunctionType.Gelu_apprx_tanh
 COPY = mybir.ActivationFunctionType.Copy
 MULT = mybir.AluOpType.mult
+ADD = mybir.AluOpType.add
 
 P = 128
-PASSES = 2
-X_PLANE = 8
+PACK = 4
+PASSES = K // (P * PACK)
+QUADRANTS = 4
+PER_COLUMN = 16
+X_FIRST = 8
+KIB = 1024
+
+SHARED_AT = {
+    "wgs": 0,
+    "xs_g1": 0,
+    "xw_g0_late": KIB // 2,
+    "xw_g10": 3 * KIB // 2,
+    "xw_g11": 7 * KIB // 2,
+    "y01": 8 * KIB,
+    "a_q2": 8 * KIB,
+    "a_bf2": 12 * KIB,
+    "y11": 12 * KIB,
+    "a_bf3": 13 * KIB,
+    "y20": 17 * KIB,
+    "we_q3": 33 * KIB // 2,
+    "a_q3": 35 * KIB // 2,
+    "we_bf3": 20 * KIB,
+    "y21": 20 * KIB,
+}
+WGS_BYTES = 4 * KIB
 
 
 def tile_moe_hie_gelu_kernel(
@@ -26,32 +50,34 @@ def tile_moe_hie_gelu_kernel(
 ):
     nc = tc.nc
     with ExitStack() as ctx:
-        sb = ctx.enter_context(tc.tile_pool(name="sb", bufs=1))
-        ps = ctx.enter_context(tc.psum_pool(name="ps", bufs=8))
+        held = ctx.enter_context(tc.tile_pool(name="held", bufs=1))
+        shared = ctx.enter_context(tc.tile_pool(name="shared", bufs=1))
+        psum = ctx.enter_context(tc.psum_pool(name="psum", bufs=8))
 
         def tile(shape, dtype, name):
-            return sb.tile(shape, dtype, name=name, align_bytes=64)
+            if name in SHARED_AT:
+                return shared.tile(shape, dtype, name=name, align_bytes=64, offset=SHARED_AT[name])
+            return held.tile(shape, dtype, name=name, align_bytes=64)
 
-        idx1 = sb.tile([P, T // 16], U16, name="idx1")
-        idx2 = sb.tile([P, T // 16], U16, name="idx2")
-        ret = sb.tile([P, T // 16], U16, name="ret")
+        def bank(shape):
+            return psum.tile(shape, F32, name="bank", tag="bank")
+
+        idx1 = held.tile([P, T // PER_COLUMN], U16, name="idx1")
+        idx2 = held.tile([P, T // PER_COLUMN], U16, name="idx2")
+        ret = held.tile([P, T // PER_COLUMN], U16, name="ret")
 
         xs = tile([P, T], U8, "xs")
-        wgs = tile([P, H], U8, "wgs")
-        nc.vector.memset(xs[:].bitcast(I32), 0)
-        nc.gpsimd.memset(wgs[:].bitcast(I32), 0)
-
-        nc.sync.dma_start(idx1[:], offs)
-        for q in range(4):
-            nc.scalar.dma_start(
-                xs[32 * q + X_PLANE : 32 * q + X_PLANE + 8, :].bitcast(I32),
-                x_scales[:, 4 * q : 4 * q + 4, :].bitcast(I32),
-            )
+        wgs = tile([P, WGS_BYTES], U8, "wgs")
+        nc.gpsimd.memset(xs[:].bitcast(I32), 0)
+        nc.gpsimd.memset(wgs[:, :H].bitcast(I32), 0)
 
         xw = [tile([P, T], I32, f"xw{s}") for s in range(PASSES)]
         wg_raw = [tile([P, PASSES * H], I32, f"wg_raw{f}") for f in range(G)]
-        we_raw = [tile([P, 4, N], F32, f"we_raw{e}") for e in range(E)]
+        we_raw = [tile([P, PACK, N], F32, f"we_raw{e}") for e in range(E)]
         g = tile([P, T], F32, "g")
+
+        def load_x(s):
+            nc.sync.dma_start(xw[s][:], x_words[s].rearrange("p t d -> p (t d)").bitcast(I32))
 
         def load_wg(f):
             nc.sync.dma_start(
@@ -60,103 +86,120 @@ def tile_moe_hie_gelu_kernel(
             )
 
         def load_we(e):
-            nc.sync.dma_start(we_raw[e][:], we[e].rearrange("(p j) n -> p j n", j=4))
+            nc.sync.dma_start(we_raw[e][:], we[e].rearrange("(p j) n -> p j n", j=PACK))
 
-        for s in range(PASSES):
-            nc.sync.dma_start(xw[s][:], x_words[s].rearrange("p t d -> p (t d)").bitcast(I32))
-        load_wg(0)
-        wgs_rows = wg_scales.rearrange("f s b i -> (f s) b i")
-        for q in range(4):
+        nc.sync.dma_start(idx1[:], offs)
+        load_x(0)
+        for q in range(QUADRANTS):
             nc.sync.dma_start(
-                wgs[32 * q : 32 * q + 16, :].bitcast(I32),
+                xs[32 * q + X_FIRST : 32 * q + X_FIRST + 4 * PASSES, :].bitcast(I32),
+                x_scales[:, 4 * q : 4 * q + 4, :].bitcast(I32),
+            )
+        load_wg(0)
+        load_x(1)
+        wgs_rows = wg_scales.rearrange("f s b i -> (f s) b i")
+        for q in range(QUADRANTS):
+            nc.sync.dma_start(
+                wgs[32 * q : 32 * q + 4 * G * PASSES, :H].bitcast(I32),
                 wgs_rows[:, 4 * q : 4 * q + 4, :].bitcast(I32),
             )
-        warm_in = tile([P, 1], F32, "warm_in")
-        warm_out = tile([P, 1], F32, "warm_out")
-        nc.vector.memset(warm_in[:], 0.0)
-        nc.scalar.activation(warm_out[:], warm_in[:], GELU)
-
         load_we(0)
         load_wg(1)
-        nc.sync.dma_start(idx2[:], offs2)
         load_we(1)
+        nc.sync.dma_start(idx2[:], offs2)
+        load_we(2)
         nc.sync.dma_start(ret[:], dst)
         nc.sync.dma_start(g[:], gate)
-        load_we(2)
         load_we(3)
 
         xs_g = [tile([P, C1], U8, f"xs_g{f}") for f in range(G)]
-        xw_g = [[tile([P, C1], U32, f"xw_g{f}{s}") for s in range(PASSES)] for f in range(G)]
+        xw_g00 = tile([P, C1], U32, "xw_g00")
+        xw_g0_early = tile([P, C2], U32, "xw_g0_early")
+        xw_g0_late = tile([P, C2], U32, "xw_g0_late")
+        xw_g0 = [[xw_g00[:, :C2], xw_g00[:, C2:]], [xw_g0_early[:], xw_g0_late[:]]]
+        xw_g1 = [tile([P, C1], U32, f"xw_g1{s}") for s in range(PASSES)]
         wg_p = [tile([P, PASSES * H], I32, f"wg_p{f}") for f in range(G)]
         wgs_p = tile([P, H], U8, "wgs_p")
-        a = tile([P, 4 * T], BF16, "a")
-        we_bf = [tile([P, N, 4], BF16, f"we_bf{e}") for e in range(E)]
-        we_q = [tile([P, N], U32, f"we_q{e}") for e in range(E)]
-        we_s = [tile([P, N], U8, f"we_s{e}") for e in range(E)]
-        a_bf = [tile([P, C2, 4], BF16, f"a_bf{e}") for e in range(E)]
+
+        a = tile([P, 2 * PACK * C1], BF16, "a")
+
+        we_bf01 = tile([P, 2 * N, PACK], BF16, "we_bf01")
+        we_q01 = tile([P, 2 * N], U32, "we_q01")
+        we_s01 = tile([P, 2 * N], U8, "we_s01")
+        we_bf = [we_bf01[:, :N, :], we_bf01[:, N:, :]]
+        we_q = [we_q01[:, :N], we_q01[:, N:]]
+        we_s = [we_s01[:, :N], we_s01[:, N:]]
+        for e in range(2, E):
+            we_bf.append(tile([P, N, PACK], BF16, f"we_bf{e}")[:])
+            we_q.append(tile([P, N], U32, f"we_q{e}")[:])
+            we_s.append(tile([P, N], U8, f"we_s{e}")[:])
+        a_bf = [tile([P, C2, PACK], BF16, f"a_bf{e}") for e in range(E)]
         a_q = [tile([P, C2], U32, f"a_q{e}") for e in range(E)]
         a_s = [tile([P, C2], U8, f"a_s{e}") for e in range(E)]
-        y = [tile([P, 2, C2], F32, f"y{e}") for e in range(E)]
-        res = [tile([P, T], F32, f"res{r}") for r in range(2)]
+        y = [[tile([P, C2], F32, f"y{e}{r}") for r in range(N // P)] for e in range(E)]
+        res = [tile([P, T], F32, f"res{r}") for r in range(N // P)]
+        y_banks = []
 
         def entries(lst, start, count):
-            return lst[:, start // 16 : (start + count) // 16]
+            return lst[:, start // PER_COLUMN : (start + count) // PER_COLUMN]
 
         def gather_scales(f):
             nc.vector.tensor_copy(xs_g[f][:], xs[:].indirect(entries(idx1, f * C1, C1)))
 
-        def gather_words(f, s, start, count):
-            nc.vector.tensor_copy(
-                xw_g[f][s][:, start : start + count],
-                xw[s][:].bitcast(U32).indirect(entries(idx1, f * C1 + start, count)),
+        def gather_words(into, s, slot, count):
+            nc.vector.tensor_copy(into, xw[s][:].bitcast(U32).indirect(entries(idx1, slot, count)))
+
+        def order_wg(f, t0, t1):
+            nc.gpsimd.tensor_copy(
+                wg_p[f][:].rearrange("p (t x) -> p t x", t=PACK)[:, t0:t1, :],
+                wg_raw[f][:].rearrange("p (x t) -> p t x", t=PACK)[:, t0:t1, :],
             )
 
-        def permute_wg(f):
-            nc.vector.tensor_copy(
-                wg_p[f][:].rearrange("p (t q l) -> p q t l", t=4, l=4),
-                wg_raw[f][:].rearrange("p (q l t) -> p q t l", t=4, l=4),
-            )
-
-        def first_pass(f, s, t, acc, start, count):
+        def first_product(f, s, t, acc, words, place, count):
             col = (t * PASSES + s) * P
             nc.tensor.matmul_mx(
                 out=acc,
                 lhsT=wg_p[f][:, col : col + P].bitcast(FP8X4),
                 lhsT_scale=wgs_p[4 * (PASSES * f + s) :, t * P : (t + 1) * P],
-                rhs=xw_g[f][s][:, start : start + count].bitcast(FP8X4),
-                rhs_scale=xs_g[f][X_PLANE + 4 * s :, start : start + count],
+                rhs=words.bitcast(FP8X4),
+                rhs_scale=xs_g[f][X_FIRST + 4 * s :, place : place + count],
                 start=(s == 0),
                 stop=(s == PASSES - 1),
             )
 
-        def cast_we(e):
+        def round_we_on_gpsimd(e):
+            nc.gpsimd.tensor_scalar(
+                we_bf[e], we_raw[e][:].rearrange("p j n -> p n j"), 1.0, 0.0, op0=MULT, op1=ADD
+            )
+
+        def round_we_on_scalar(e):
             nc.scalar.copy(
-                we_bf[e][:].rearrange("p (c i) j -> p c j i", i=4),
+                we_bf[e].rearrange("p (c i) j -> p c j i", i=4),
                 we_raw[e][:].rearrange("p j (c i) -> p c j i", i=4),
             )
 
         def quantize(codes, scales, values):
             nc.vector.quantize_mx(
-                out=codes[:].bitcast(FP8X4), scales=scales[:], in_=values[:].rearrange("p n j -> p (n j)")
+                out=codes.bitcast(FP8X4), scales=scales, in_=values.rearrange("p n j -> p (n j)")
             )
 
-        def gather_pairs(e):
-            for u in range(2):
-                words = a_bf[e][:].rearrange("p n j -> p (n j)").bitcast(U32)
-                nc.vector.tensor_copy(
-                    words[:, u :: 2],
-                    a[:, u * 2 * C1 : (u + 1) * 2 * C1].bitcast(U32).indirect(entries(idx2, e * C2, C2)),
-                )
+        def quantize_a(e):
+            quantize(a_q[e][:], a_s[e][:], a_bf[e][:])
+
+        def gather_pairs(e, u):
+            as_pairs = a_bf[e][:].rearrange("p n j -> p (n j)").bitcast(U32)
+            window = a[:, u * 2 * C1 : (u + 1) * 2 * C1].bitcast(U32)
+            nc.vector.tensor_copy(as_pairs[:, u::2], window.indirect(entries(idx2, e * C2, C2)))
 
         def gather_plane(e, t):
-            lo = 3 * C1 + t * C1
+            lo = (PACK + t - 1) * C1
             nc.scalar.activation(
                 a_bf[e][:, :, t], a[:, lo : lo + T].indirect(entries(idx2, e * C2, C2)), COPY
             )
 
-        def second(e):
-            acc = ps.tile([P, 2, C2], F32, name="acc", tag="bank")
-            for r in range(2):
+        def second_product(e):
+            acc = bank([P, N // P, C2])
+            for r in range(N // P):
                 nc.tensor.matmul_mx(
                     out=acc[:, r, :],
                     lhsT=we_q[e][:, r * P : (r + 1) * P].bitcast(FP8X4),
@@ -166,65 +209,91 @@ def tile_moe_hie_gelu_kernel(
                     start=True,
                     stop=True,
                 )
-            nc.scalar.copy(y[e][:], acc[:])
+            y_banks.append(acc)
+
+        def leave_psum(e, r):
+            nc.scalar.copy(y[e][r][:], y_banks[e][:, r, :])
 
         def scatter(e, r):
             nc.vector.tensor_tensor(
-                res[r][:].indirect(entries(ret, e * C2, C2)), y[e][:, r, :], g[:, e * C2 : (e + 1) * C2], MULT
+                res[r][:].indirect(entries(ret, e * C2, C2)), y[e][r][:], g[:, e * C2 : (e + 1) * C2], MULT
             )
 
+        gather_words(xw_g00[:], 0, 0, C1)
         gather_scales(0)
-        gather_scales(1)
-        gather_words(0, 0, 0, C1)
-        gather_words(0, 1, 0, C2)
+        order_wg(0, 0, 2)
+        order_wg(0, 2, PACK)
+        gather_words(xw_g0[1][0], 1, 0, C2)
         nc.vector.tensor_copy(
-            wgs_p[:].rearrange("p (t m) -> p t m", t=4), wgs[:].rearrange("p (m t) -> p t m", t=4)
+            wgs_p[:].rearrange("p (t m) -> p t m", t=PACK), wgs[:, :H].rearrange("p (m t) -> p t m", t=PACK)
         )
-        permute_wg(0)
-        gather_words(0, 1, C2, C2)
-        cast_we(0)
-        for h in range(2):
-            for u in range(2):
-                acc = ps.tile([P, 2, C2], F32, name="acc", tag="bank")
+        gather_words(xw_g0[1][1], 1, C2, C2)
+        round_we_on_gpsimd(0)
+        for u in range(2):
+            for h in range(2):
+                acc = bank([P, 2, C2])
                 for c in range(2):
                     for s in range(PASSES):
-                        first_pass(0, s, 2 * u + c, acc[:, c, :], h * C2, C2)
+                        first_product(0, s, 2 * u + c, acc[:, c, :], xw_g0[s][h], h * C2, C2)
                 lo = u * 2 * C1 + h * 2 * C2
                 nc.scalar.activation(
                     a[:, lo : lo + 2 * C2].rearrange("p (n c) -> p n c", c=2),
                     acc[:].rearrange("p c n -> p n c"),
                     GELU,
                 )
-        gather_words(1, 0, 0, C1)
-        permute_wg(1)
-        gather_words(1, 1, 0, C1)
-        cast_we(1)
-        banks = [ps.tile([P, C1], F32, name="acc", tag="bank") for t in range(4)]
+
+        gather_scales(1)
+        gather_words(xw_g1[0][:], 0, C1, C1)
+        order_wg(1, 0, PACK)
+        gather_words(xw_g1[1][:], 1, C1, C1)
+        round_we_on_gpsimd(1)
+        planes = [bank([P, C1]) for t in range(PACK)]
         for s in range(PASSES):
-            for t in range(4):
-                first_pass(1, s, t, banks[t][:], 0, C1)
-        quantize(we_q[0], we_s[0], we_bf[0])
-        gather_pairs(0)
-        quantize(we_q[1], we_s[1], we_bf[1])
-        quantize(a_q[0], a_s[0], a_bf[0])
-        for t in range(4):
-            lo = 4 * C1 + t * C1
-            nc.scalar.activation(a[:, lo : lo + C1], banks[t][:], GELU)
-        second(0)
-        gather_pairs(1)
+            for t in range(PACK):
+                first_product(1, s, t, planes[t][:], xw_g1[s][:], 0, C1)
+
+        gather_pairs(0, 0)
+        gather_pairs(1, 0)
+        gather_pairs(0, 1)
+        quantize(we_q01[:], we_s01[:], we_bf01[:])
+        quantize_a(0)
+        for t in range(PACK):
+            lo = (PACK + t) * C1
+            nc.scalar.activation(a[:, lo : lo + C1], planes[t][:], GELU)
+        second_product(0)
+        leave_psum(0, 0)
+        leave_psum(0, 1)
+        gather_pairs(1, 1)
+        quantize_a(1)
+        second_product(1)
         scatter(0, 0)
-        quantize(a_q[1], a_s[1], a_bf[1])
-        second(1)
+        leave_psum(1, 0)
         scatter(0, 1)
-        for e in range(2, E):
-            cast_we(e)
-            for t in range(4):
-                gather_plane(e, t)
-            quantize(we_q[e], we_s[e], we_bf[e])
-            quantize(a_q[e], a_s[e], a_bf[e])
-            second(e)
-            scatter(e - 1, 0)
-            scatter(e - 1, 1)
-        for r in range(2):
-            scatter(E - 1, r)
-            nc.sync.dma_start(out[r * P : (r + 1) * P, :], res[r][:])
+
+        scatter(1, 0)
+        for t in range(PACK):
+            gather_plane(2, t)
+        round_we_on_gpsimd(2)
+        round_we_on_scalar(3)
+        quantize_a(2)
+        quantize(we_q[2], we_s[2], we_bf[2])
+        leave_psum(1, 1)
+        second_product(2)
+        leave_psum(2, 0)
+        scatter(1, 1)
+
+        scatter(2, 0)
+        for t in range(PACK):
+            gather_plane(3, t)
+        quantize(we_q[3], we_s[3], we_bf[3])
+        quantize_a(3)
+        leave_psum(2, 1)
+        second_product(3)
+        leave_psum(3, 0)
+        scatter(2, 1)
+
+        scatter(3, 0)
+        nc.sync.dma_start(out[:P, :], res[0][:])
+        leave_psum(3, 1)
+        scatter(3, 1)
+        nc.sync.dma_start(out[P:, :], res[1][:])

from contextlib import ExitStack

import concourse.mybir as mybir

K, T, G, C1, E, C2, H, N = 1024, 1024, 2, 512, 4, 256, 512, 256
FLOPS = 2 * T * (K * H + H * N)

F32 = mybir.dt.float32
BF16 = mybir.dt.bfloat16
I32 = mybir.dt.int32
U32 = mybir.dt.uint32
U16 = mybir.dt.uint16
U8 = mybir.dt.uint8
FP8X4 = mybir.dt.float8_e4m3fn_x4
GELU = mybir.ActivationFunctionType.Gelu_apprx_tanh
COPY = mybir.ActivationFunctionType.Copy
MULT = mybir.AluOpType.mult
ADD = mybir.AluOpType.add

P = 128
PACK = 4
PASSES = K // (P * PACK)
QUADRANTS = 4
PER_COLUMN = 16
X_FIRST = 8
KIB = 1024

SHARED_AT = {
    "wgs": 0,
    "xs_g1": 0,
    "xw_g0_late": KIB // 2,
    "xw_g10": 3 * KIB // 2,
    "xw_g11": 7 * KIB // 2,
    "y01": 8 * KIB,
    "a_q2": 8 * KIB,
    "a_bf2": 12 * KIB,
    "y11": 12 * KIB,
    "a_bf3": 13 * KIB,
    "y20": 17 * KIB,
    "we_q3": 33 * KIB // 2,
    "a_q3": 35 * KIB // 2,
    "we_bf3": 20 * KIB,
    "y21": 20 * KIB,
}
WGS_BYTES = 4 * KIB


def tile_moe_hie_gelu_kernel(
    tc, x_words, x_scales, wg_words, wg_scales, we, gate, offs, offs2, dst, out
):
    nc = tc.nc
    with ExitStack() as ctx:
        held = ctx.enter_context(tc.tile_pool(name="held", bufs=1))
        shared = ctx.enter_context(tc.tile_pool(name="shared", bufs=1))
        psum = ctx.enter_context(tc.psum_pool(name="psum", bufs=8))

        def tile(shape, dtype, name):
            if name in SHARED_AT:
                return shared.tile(shape, dtype, name=name, align_bytes=64, offset=SHARED_AT[name])
            return held.tile(shape, dtype, name=name, align_bytes=64)

        def bank(shape):
            return psum.tile(shape, F32, name="bank", tag="bank")

        idx1 = held.tile([P, T // PER_COLUMN], U16, name="idx1")
        idx2 = held.tile([P, T // PER_COLUMN], U16, name="idx2")
        ret = held.tile([P, T // PER_COLUMN], U16, name="ret")

        xs = tile([P, T], U8, "xs")
        wgs = tile([P, WGS_BYTES], U8, "wgs")
        nc.gpsimd.memset(xs[:].bitcast(I32), 0)
        nc.gpsimd.memset(wgs[:, :H].bitcast(I32), 0)

        xw = [tile([P, T], I32, f"xw{s}") for s in range(PASSES)]
        wg_raw = [tile([P, PASSES * H], I32, f"wg_raw{f}") for f in range(G)]
        we_raw = [tile([P, PACK, N], F32, f"we_raw{e}") for e in range(E)]
        g = tile([P, T], F32, "g")

        def load_x(s):
            nc.sync.dma_start(xw[s][:], x_words[s].rearrange("p t d -> p (t d)").bitcast(I32))

        def load_wg(f):
            nc.sync.dma_start(
                wg_raw[f][:].rearrange("p (s i) -> p s i", s=PASSES),
                wg_words[f].rearrange("s p i d -> p s (i d)").bitcast(I32),
            )

        def load_we(e):
            nc.sync.dma_start(we_raw[e][:], we[e].rearrange("(p j) n -> p j n", j=PACK))

        nc.sync.dma_start(idx1[:], offs)
        load_x(0)
        for q in range(QUADRANTS):
            nc.sync.dma_start(
                xs[32 * q + X_FIRST : 32 * q + X_FIRST + 4 * PASSES, :].bitcast(I32),
                x_scales[:, 4 * q : 4 * q + 4, :].bitcast(I32),
            )
        load_wg(0)
        load_x(1)
        wgs_rows = wg_scales.rearrange("f s b i -> (f s) b i")
        for q in range(QUADRANTS):
            nc.sync.dma_start(
                wgs[32 * q : 32 * q + 4 * G * PASSES, :H].bitcast(I32),
                wgs_rows[:, 4 * q : 4 * q + 4, :].bitcast(I32),
            )
        load_we(0)
        load_wg(1)
        load_we(1)
        nc.sync.dma_start(idx2[:], offs2)
        load_we(2)
        nc.sync.dma_start(ret[:], dst)
        nc.sync.dma_start(g[:], gate)
        load_we(3)

        xs_g = [tile([P, C1], U8, f"xs_g{f}") for f in range(G)]
        xw_g00 = tile([P, C1], U32, "xw_g00")
        xw_g0_early = tile([P, C2], U32, "xw_g0_early")
        xw_g0_late = tile([P, C2], U32, "xw_g0_late")
        xw_g0 = [[xw_g00[:, :C2], xw_g00[:, C2:]], [xw_g0_early[:], xw_g0_late[:]]]
        xw_g1 = [tile([P, C1], U32, f"xw_g1{s}") for s in range(PASSES)]
        wg_p = [tile([P, PASSES * H], I32, f"wg_p{f}") for f in range(G)]
        wgs_p = tile([P, H], U8, "wgs_p")

        a = tile([P, 2 * PACK * C1], BF16, "a")

        we_bf01 = tile([P, 2 * N, PACK], BF16, "we_bf01")
        we_q01 = tile([P, 2 * N], U32, "we_q01")
        we_s01 = tile([P, 2 * N], U8, "we_s01")
        we_bf = [we_bf01[:, :N, :], we_bf01[:, N:, :]]
        we_q = [we_q01[:, :N], we_q01[:, N:]]
        we_s = [we_s01[:, :N], we_s01[:, N:]]
        for e in range(2, E):
            we_bf.append(tile([P, N, PACK], BF16, f"we_bf{e}")[:])
            we_q.append(tile([P, N], U32, f"we_q{e}")[:])
            we_s.append(tile([P, N], U8, f"we_s{e}")[:])
        a_bf = [tile([P, C2, PACK], BF16, f"a_bf{e}") for e in range(E)]
        a_q = [tile([P, C2], U32, f"a_q{e}") for e in range(E)]
        a_s = [tile([P, C2], U8, f"a_s{e}") for e in range(E)]
        y = [[tile([P, C2], F32, f"y{e}{r}") for r in range(N // P)] for e in range(E)]
        res = [tile([P, T], F32, f"res{r}") for r in range(N // P)]
        y_banks = []

        def entries(lst, start, count):
            return lst[:, start // PER_COLUMN : (start + count) // PER_COLUMN]

        def gather_scales(f):
            nc.vector.tensor_copy(xs_g[f][:], xs[:].indirect(entries(idx1, f * C1, C1)))

        def gather_words(into, s, slot, count):
            nc.vector.tensor_copy(into, xw[s][:].bitcast(U32).indirect(entries(idx1, slot, count)))

        def order_wg(f, t0, t1):
            nc.gpsimd.tensor_copy(
                wg_p[f][:].rearrange("p (t x) -> p t x", t=PACK)[:, t0:t1, :],
                wg_raw[f][:].rearrange("p (x t) -> p t x", t=PACK)[:, t0:t1, :],
            )

        def first_product(f, s, t, acc, words, place, count):
            col = (t * PASSES + s) * P
            nc.tensor.matmul_mx(
                out=acc,
                lhsT=wg_p[f][:, col : col + P].bitcast(FP8X4),
                lhsT_scale=wgs_p[4 * (PASSES * f + s) :, t * P : (t + 1) * P],
                rhs=words.bitcast(FP8X4),
                rhs_scale=xs_g[f][X_FIRST + 4 * s :, place : place + count],
                start=(s == 0),
                stop=(s == PASSES - 1),
            )

        def round_we_on_gpsimd(e):
            nc.gpsimd.tensor_scalar(
                we_bf[e], we_raw[e][:].rearrange("p j n -> p n j"), 1.0, 0.0, op0=MULT, op1=ADD
            )

        def round_we_on_scalar(e):
            nc.scalar.copy(
                we_bf[e].rearrange("p (c i) j -> p c j i", i=4),
                we_raw[e][:].rearrange("p j (c i) -> p c j i", i=4),
            )

        def quantize(codes, scales, values):
            nc.vector.quantize_mx(
                out=codes.bitcast(FP8X4), scales=scales, in_=values.rearrange("p n j -> p (n j)")
            )

        def quantize_a(e):
            quantize(a_q[e][:], a_s[e][:], a_bf[e][:])

        def gather_pairs(e, u):
            as_pairs = a_bf[e][:].rearrange("p n j -> p (n j)").bitcast(U32)
            window = a[:, u * 2 * C1 : (u + 1) * 2 * C1].bitcast(U32)
            nc.vector.tensor_copy(as_pairs[:, u::2], window.indirect(entries(idx2, e * C2, C2)))

        def gather_plane(e, t):
            lo = (PACK + t - 1) * C1
            nc.scalar.activation(
                a_bf[e][:, :, t], a[:, lo : lo + T].indirect(entries(idx2, e * C2, C2)), COPY
            )

        def second_product(e):
            acc = bank([P, N // P, C2])
            for r in range(N // P):
                nc.tensor.matmul_mx(
                    out=acc[:, r, :],
                    lhsT=we_q[e][:, r * P : (r + 1) * P].bitcast(FP8X4),
                    lhsT_scale=we_s[e][:, r * P : (r + 1) * P],
                    rhs=a_q[e][:].bitcast(FP8X4),
                    rhs_scale=a_s[e][:],
                    start=True,
                    stop=True,
                )
            y_banks.append(acc)

        def leave_psum(e, r):
            nc.scalar.copy(y[e][r][:], y_banks[e][:, r, :])

        def scatter(e, r):
            nc.vector.tensor_tensor(
                res[r][:].indirect(entries(ret, e * C2, C2)), y[e][r][:], g[:, e * C2 : (e + 1) * C2], MULT
            )

        gather_words(xw_g00[:], 0, 0, C1)
        gather_scales(0)
        order_wg(0, 0, 2)
        order_wg(0, 2, PACK)
        gather_words(xw_g0[1][0], 1, 0, C2)
        nc.vector.tensor_copy(
            wgs_p[:].rearrange("p (t m) -> p t m", t=PACK), wgs[:, :H].rearrange("p (m t) -> p t m", t=PACK)
        )
        gather_words(xw_g0[1][1], 1, C2, C2)
        round_we_on_gpsimd(0)
        for u in range(2):
            for h in range(2):
                acc = bank([P, 2, C2])
                for c in range(2):
                    for s in range(PASSES):
                        first_product(0, s, 2 * u + c, acc[:, c, :], xw_g0[s][h], h * C2, C2)
                lo = u * 2 * C1 + h * 2 * C2
                nc.scalar.activation(
                    a[:, lo : lo + 2 * C2].rearrange("p (n c) -> p n c", c=2),
                    acc[:].rearrange("p c n -> p n c"),
                    GELU,
                )

        gather_scales(1)
        gather_words(xw_g1[0][:], 0, C1, C1)
        order_wg(1, 0, PACK)
        gather_words(xw_g1[1][:], 1, C1, C1)
        round_we_on_gpsimd(1)
        planes = [bank([P, C1]) for t in range(PACK)]
        for s in range(PASSES):
            for t in range(PACK):
                first_product(1, s, t, planes[t][:], xw_g1[s][:], 0, C1)

        gather_pairs(0, 0)
        gather_pairs(1, 0)
        gather_pairs(0, 1)
        quantize(we_q01[:], we_s01[:], we_bf01[:])
        quantize_a(0)
        for t in range(PACK):
            lo = (PACK + t) * C1
            nc.scalar.activation(a[:, lo : lo + C1], planes[t][:], GELU)
        second_product(0)
        leave_psum(0, 0)
        leave_psum(0, 1)
        gather_pairs(1, 1)
        quantize_a(1)
        second_product(1)
        scatter(0, 0)
        leave_psum(1, 0)
        scatter(0, 1)

        scatter(1, 0)
        for t in range(PACK):
            gather_plane(2, t)
        round_we_on_gpsimd(2)
        round_we_on_scalar(3)
        quantize_a(2)
        quantize(we_q[2], we_s[2], we_bf[2])
        leave_psum(1, 1)
        second_product(2)
        leave_psum(2, 0)
        scatter(1, 1)

        scatter(2, 0)
        for t in range(PACK):
            gather_plane(3, t)
        quantize(we_q[3], we_s[3], we_bf[3])
        quantize_a(3)
        leave_psum(2, 1)
        second_product(3)
        leave_psum(3, 0)
        scatter(2, 1)

        scatter(3, 0)
        nc.sync.dma_start(out[:P, :], res[0][:])
        leave_psum(3, 1)
        scatter(3, 1)
        nc.sync.dma_start(out[P:, :], res[1][:])
